import numpy as np
import ml_dtypes


def mxq(x, axis, fmt="e4m3"):
    dtype, down = {"e4m3": (ml_dtypes.float8_e4m3fn, 7), "e5m2": (ml_dtypes.float8_e5m2, 14)}[fmt]
    v = np.moveaxis(np.asarray(x, np.float32).astype(ml_dtypes.bfloat16).astype(np.float64), axis, -1)
    blocks = v.reshape(v.shape[:-1] + (-1, 32))
    amax = np.abs(blocks).max(-1, keepdims=True)
    byte = np.maximum(np.where(amax > 0, np.frexp(amax)[1] - 1 + 127, 0) - down, 1)
    scale = np.exp2(byte - 127.0)
    codes = (blocks / scale).astype(np.float32).astype(dtype).astype(np.float64)
    return np.moveaxis((codes * scale).reshape(v.shape), -1, axis)


WIDE = False


def mx_kscale(k):
    if not WIDE:
        return np.ones(k)
    levels = np.array([10, -10, 5, -5, 0])
    if k % 512:
        return np.exp2(np.random.permutation(np.resize(levels, k // 32))).repeat(32)
    a = np.empty((k // 512, 16))
    for p in range(k // 512):
        a[p, :8] = np.random.permutation(np.resize(levels, 8))
        for g in range(8):
            far = levels[np.abs(levels - a[p, g]) >= 10]
            a[p, g + 8] = far[np.random.randint(len(far))]
    return np.exp2(a.ravel()).repeat(32)


def f64(x):
    return np.asarray(x).astype(np.float64)


def striped(idx):
    return np.tile(np.asarray(idx).reshape(-1, 16).T, (8, 1)).astype(np.uint16)


def unstriped(offs):
    return offs[:16].T.reshape(-1).astype(np.int64)


def striped8(idx):
    return np.asarray(idx).reshape(8, -1, 16).transpose(0, 2, 1).reshape(128, -1).astype(np.uint16)


def unstriped8(offs):
    return offs.reshape(8, 16, -1).transpose(0, 2, 1).reshape(8, -1).astype(np.int64)


def pick8(x, idx, run):
    r = np.arange(len(x))
    return x[r[:, None], idx[r % (8 * run) // run]]


E2M1 = np.array([0.0, 0.5, 1.0, 1.5, 2.0, 3.0, 4.0, 6.0, -0.0, -0.5, -1.0, -1.5, -2.0, -3.0, -4.0, -6.0])


def pack_weight(w, fmt):
    k, n = w.shape
    w = f64(np.asarray(w, np.float32).astype(ml_dtypes.bfloat16)).reshape(k // 32, 32, n)
    amax = np.abs(w).max(1)
    if fmt == "e4m3":
        byte = np.frexp(amax)[1] - 1 + 127 - 7
    else:
        mant, ex = np.frexp(amax / 6.0)
        byte = np.where(mant > 0.5, ex, ex - 1) + 127
    byte = np.clip(np.where(amax > 0, byte, 1), 1, 254)
    scaled = (w * np.exp2(127.0 - byte)[:, None, :]).reshape(k, n).astype(np.float32)
    by_word = np.ascontiguousarray(scaled.reshape(k // 512, 128, 4, n).transpose(0, 1, 3, 2))
    if fmt == "e4m3":
        words = by_word.astype(ml_dtypes.float8_e4m3fn).view(np.uint8)
    else:
        c = by_word.astype(ml_dtypes.float4_e2m1fn).view(np.uint8) & 0xF
        words = (c[..., 0::2] | (c[..., 1::2] << 4)).reshape(k // 512, 128, 2 * n)
    return np.ascontiguousarray(words), np.ascontiguousarray(byte.astype(np.uint8).reshape(k // 512, 16, n))


def unpack_weight(words, scales, fmt):
    g, _, n = scales.shape
    words = np.ascontiguousarray(words).reshape(g, 128, n, -1)
    if fmt == "e4m3":
        vals = words.view(ml_dtypes.float8_e4m3fn).astype(np.float64)
    else:
        nib = np.empty((g, 128, n, 4), np.uint8)
        nib[..., 0::2] = words & 0xF
        nib[..., 1::2] = words >> 4
        vals = E2M1[nib]
    vals = vals * np.repeat(np.exp2(scales.astype(np.float64) - 127.0), 8, axis=1)[..., None]
    return vals.transpose(0, 1, 3, 2).reshape(g * 512, n)


K, J, R, T, U, F, C, O, N = 512, 256, 512, 512, 512, 1024, 512, 128, 256


def setup_inputs():
    n = np.random.standard_normal
    idx = np.stack([np.random.permutation(T)[:J] for _ in range(8)])
    idx2 = np.stack([np.random.permutation(U)[:J] for _ in range(8)])
    idx3 = np.stack([np.random.permutation(U)[:J] for _ in range(8)])
    idx4 = np.random.permutation(F)[:R]
    idx5 = np.random.permutation(C)[:J]
    idx6 = np.random.permutation(C)[:O]
    idx7 = np.stack([np.random.permutation(C)[:O] for _ in range(8)])
    fk = mx_kscale(K)
    fr = mx_kscale(R)
    tr = np.ones(F)
    tr[idx4] = fr
    wtp = pack_weight(n((K, F)) * 1 / np.sqrt(K) / fk[:, None] * tr, "e2m1")
    wbp = pack_weight(n((R, N)) * 1 / np.sqrt(R) / fr[:, None], "e4m3")
    return {
        "ta": (np.random.randint(-7, 8, (K, T)).astype(np.float64)).astype(np.float32),
        "tb": (np.random.randint(-7, 8, (K, U)).astype(np.float64)).astype(np.float32),
        "ga": ((np.random.randint(8, 25, (K, 1)) / 64.0) * fk[:, None]).astype(np.float32),
        "gb": ((np.random.randint(8, 25, (K, 1)) / 64.0) * fk[:, None]).astype(np.float32),
        "gd": ((np.random.randint(8, 25, (K, 1)) / 64.0) * fk[:, None]).astype(np.float32),
        "wt_words": wtp[0],
        "wt_scales": wtp[1],
        "sa": (np.random.uniform(0.5, 1.6, (R, 1))).astype(np.float32),
        "sb": (np.random.uniform(0.5, 1.6, (R, 1))).astype(np.float32),
        "wb_words": wbp[0],
        "wb_scales": wbp[1],
        "offs": striped8(idx),
        "offs2": striped8(idx2),
        "offs3": striped8(idx3),
        "offs4": striped(idx4),
        "offs5": striped(idx5),
        "offs6": striped(idx6),
        "offs7": striped8(idx7),
    }


def reference(ta, tb, ga, gb, gd, wt_words, wt_scales, sa, sb, wb_words, wb_scales, offs, offs2, offs3, offs4, offs5, offs6, offs7):
    idx = unstriped8(offs)
    idx2 = unstriped8(offs2)
    idx3 = unstriped8(offs3)
    idx4 = unstriped(offs4)
    idx5 = unstriped(offs5)
    idx6 = unstriped(offs6)
    idx7 = unstriped8(offs7)
    wtu = unpack_weight(wt_words, wt_scales, "e2m1")
    wbu = unpack_weight(wb_words, wb_scales, "e4m3")
    xc = np.maximum(np.minimum(pick8(f64(ta), idx, 64) * f64(ga), pick8(f64(tb), idx2, 64) * f64(gb)), pick8(f64(tb), idx3, 64) * f64(gd))
    wtidx4g = wtu[:, idx4]
    xcq = mxq(xc, 0, "e4m3")
    a = wtidx4g.T @ xcq
    pw = np.zeros((R, C))
    pw[:, idx5] = a
    hid = np.maximum(pw[:, idx6] * f64(sa), pick8(pw, idx7, 64) * f64(sb))
    hidq = mxq(hid, 0, "e4m3")
    y = wbu.T @ hidq
    return y

@@ -1,0 +1,235 @@
+from contextlib import ExitStack
+
+import concourse.mybir as mybir
+
+K, J, R, T, F, C, O, N = 512, 256, 512, 512, 1024, 512, 128, 256
+FLOPS = 2 * K * R * J + 2 * R * N * O
+
+F32 = mybir.dt.float32
+BF16 = mybir.dt.bfloat16
+I32 = mybir.dt.int32
+U32 = mybir.dt.uint32
+U16 = mybir.dt.uint16
+U8 = mybir.dt.uint8
+FP8X4 = mybir.dt.float8_e4m3fn_x4
+FP4X4 = mybir.dt.float4_e2m1fn_x4
+COPY = mybir.ActivationFunctionType.Copy
+MIN = mybir.AluOpType.min
+MAX = mybir.AluOpType.max
+
+P = 128
+PACK = 4
+HALF = J // 2
+LIST_ROWS = 16
+
+
+def tile_picked_boundedcode_store_one_boardmixed_one_plain_kernel(
+    tc, ta, tb, ga, gb, gd, wt_words, wt_scales, sa, sb, wb_words, wb_scales,
+    offs, offs2, offs3, offs4, offs5, offs6, offs7, out,
+):
+    nc = tc.nc
+    with ExitStack() as ctx:
+        keep = ctx.enter_context(tc.tile_pool(name="keep", bufs=1))
+        psum = ctx.enter_context(tc.psum_pool(name="psum", bufs=1))
+
+        def load_list(name, src):
+            tile = keep.tile(list(src.shape), U16, name=name)
+            nc.sync.dma_start(tile[:], src)
+            return tile
+
+        def load_factors(name, src, queue=nc.sync):
+            tile = keep.tile([P, PACK], F32, name=name)
+            queue.dma_start(tile[:], src.rearrange("(p t) o -> p (t o)", t=PACK))
+            return tile
+
+        def load_rows(name, src, t, queue=nc.sync):
+            tile = keep.tile([P, T], F32, name=name + str(t))
+            queue.dma_start(tile[:], src.rearrange("(p t) c -> p t c", t=PACK)[:, t, :])
+            return tile
+
+        wt_scale_window = keep.tile([P, F], U8, name="wt_scale_window")
+        wb_scale = keep.tile([P, N], U8, name="wb_scale", align_bytes=64)
+        nc.vector.memset(wt_scale_window[:].bitcast(I32), 0)
+        nc.vector.memset(wb_scale[:].bitcast(I32), 0)
+
+        ta_rows, tb_rows = {}, {}
+        code_list = load_list("code_list", offs)
+        ga_sb = load_factors("ga_sb", ga)
+        ta_rows[0] = load_rows("ta_rows", ta, 0, nc.scalar)
+        wt_scale_stage = keep.tile([4, 4, F // 4], I32, name="wt_scale_stage")
+        nc.gpsimd.dma_start(wt_scale_stage[:], wt_scales[0].bitcast(I32).rearrange("(q r) c -> r q c", r=4))
+        upper_list = load_list("upper_list", offs2)
+        gb_sb = load_factors("gb_sb", gb)
+        tb_rows[0] = load_rows("tb_rows", tb, 0)
+        store_list = load_list("store_list", offs4)
+        wt_word_window = keep.tile([P, F], U16, name="wt_word_window")
+        nc.sync.dma_start(wt_word_window[:].bitcast(I32), wt_words[0].bitcast(I32))
+        ta_rows[1] = load_rows("ta_rows", ta, 1)
+        lower_list = load_list("lower_list", offs3)
+        gd_sb = load_factors("gd_sb", gd)
+        tb_rows[1] = load_rows("tb_rows", tb, 1)
+        for t in (2, 3):
+            ta_rows[t] = load_rows("ta_rows", ta, t)
+            tb_rows[t] = load_rows("tb_rows", tb, t)
+        board_list = load_list("board_list", offs5)
+        first_list = load_list("first_list", offs6)
+        second_list = load_list("second_list", offs7)
+        sa_sb = load_factors("sa_sb", sa)
+        sb_sb = load_factors("sb_sb", sb)
+        wb_codes = keep.tile([P, N], U32, name="wb_codes", align_bytes=64)
+        nc.sync.dma_start(wb_codes[:].bitcast(I32), wb_words[0].rearrange("p n r -> p (n r)").bitcast(I32))
+        for q in range(4):
+            nc.sync.dma_start(
+                wb_scale[32 * q : 32 * q + 4, :].bitcast(I32), wb_scales[0, 4 * q : 4 * q + 4, :].bitcast(I32)
+            )
+
+        board = [keep.tile([P, C], F32, name="board" + str(t)) for t in range(PACK)]
+        for t in range(PACK):
+            nc.vector.memset(board[t][:], 0.0)
+
+        def fetch(dst, window, offsets, factor):
+            nc.scalar.activation(out=dst, in_=window[:].indirect(offsets), func=COPY, scale=factor)
+
+        def half_of(lst, h):
+            cols = HALF // LIST_ROWS
+            return lst[:, h * cols : (h + 1) * cols]
+
+        def slots(h):
+            return slice(h * HALF, (h + 1) * HALF)
+
+        def pair_tile(name):
+            return keep.tile([P, 2, HALF], F32, name=name)
+
+        def code_and_upper(t, h, code, upper, least):
+            fetch(code, ta_rows[t], half_of(code_list, h), ga_sb[:, t : t + 1])
+            fetch(upper, tb_rows[t], half_of(upper_list, h), gb_sb[:, t : t + 1])
+            nc.vector.tensor_tensor(least, code, upper, MIN)
+
+        def lower(t, h, dst):
+            fetch(dst, tb_rows[t], half_of(lower_list, h), gd_sb[:, t : t + 1])
+
+        def larger_pair(dst, pair, x, y):
+            nc.vector.tensor_tensor(
+                dst[:, :, 2 * pair : 2 * pair + 2], x.rearrange("p t j -> p j t"), y.rearrange("p t j -> p j t"), MAX
+            )
+
+        def quantise(name, src):
+            codes = keep.tile([P, HALF], U32, name=name + "_codes", align_bytes=64)
+            scale = keep.tile([P, HALF], U8, name=name + "_scale", align_bytes=64)
+            nc.vector.quantize_mx(out=codes[:].bitcast(FP8X4), scales=scale[:], in_=src[:].rearrange("p j t -> p (j t)"))
+            return codes, scale
+
+        wt_picked = keep.tile([P, R], U16, name="wt_picked")
+        wt_codes = keep.tile([P, R], U16, name="wt_codes", align_bytes=64)
+        wt_scale = keep.tile([P, R], U8, name="wt_scale", align_bytes=64)
+
+        def hidden_product(h, grouped, sums, order):
+            codes, scale = quantise("xc" + str(h), grouped)
+            for t in order:
+                nc.tensor.matmul_mx(
+                    out=sums[t],
+                    lhsT=wt_codes[:, P * t : P * (t + 1)].bitcast(FP4X4),
+                    lhsT_scale=wt_scale[:, P * t : P * (t + 1)],
+                    rhs=codes[:].bitcast(FP8X4),
+                    rhs_scale=scale[:],
+                    start=True,
+                    stop=True,
+                )
+
+        def put_vector(t, h, values):
+            nc.vector.tensor_copy(board[t][:].indirect(half_of(board_list, h)), values)
+
+        def put_scalar(t, h, values):
+            nc.scalar.activation(out=board[t][:].indirect(half_of(board_list, h)), in_=values, func=COPY)
+
+        def bank(name, planes):
+            return psum.tile([P, planes, HALF], F32, name=name)
+
+        least01 = keep.tile([P, 2, J], F32, name="least01")
+        grouped = keep.tile([P, HALF, PACK], BF16, name="grouped", align_bytes=64)
+
+        for q in range(4):
+            nc.vector.tensor_copy(wt_scale_window[32 * q : 32 * q + 4, :].bitcast(I32), wt_scale_stage[:, q, :])
+        nc.vector.tensor_copy(
+            wt_scale[:].rearrange("p (t m) -> p m t", t=PACK), wt_scale_window[:].indirect(store_list[:])
+        )
+        nc.vector.tensor_copy(wt_picked[:], wt_word_window[:].indirect(store_list[:]))
+
+        code0 = keep.tile([P, J], F32, name="code0")
+        upper0 = keep.tile([P, J], F32, name="upper0")
+        lower01 = keep.tile([P, 2, J], F32, name="lower01")
+        fetch(code0[:], ta_rows[0], code_list[:], ga_sb[:, 0:1])
+        fetch(upper0[:], tb_rows[0], upper_list[:], gb_sb[:, 0:1])
+        fetch(lower01[:, 0, :], tb_rows[0], lower_list[:], gd_sb[:, 0:1])
+        nc.vector.tensor_tensor(least01[:, 0, :], code0[:], upper0[:], MIN)
+        nc.vector.tensor_copy(
+            wt_codes[:].rearrange("p (t m) -> p t m", t=PACK), wt_picked[:].rearrange("p (m t) -> p t m", t=PACK)
+        )
+        buf_x, buf_y, buf_z = pair_tile("buf_x"), pair_tile("buf_y"), pair_tile("buf_z")
+        both1, both2 = pair_tile("both1"), pair_tile("both2")
+        code_and_upper(1, 0, both1[:, 0, :], both1[:, 1, :], least01[:, 1, slots(0)])
+        fetch(lower01[:, 1, :], tb_rows[1], lower_list[:], gd_sb[:, 1:2])
+        larger_pair(grouped, 0, least01[:, :, slots(0)], lower01[:, :, slots(0)])
+        code_and_upper(2, 0, both2[:, 0, :], both2[:, 1, :], buf_z[:, 0, :])
+        lower(2, 0, buf_y[:, 0, :])
+        code_and_upper(3, 0, buf_x[:, 0, :], buf_x[:, 1, :], buf_z[:, 1, :])
+        lower(3, 0, buf_y[:, 1, :])
+        larger_pair(grouped, 1, buf_z[:], buf_y[:])
+        a0, a123 = bank("a0", 1), bank("a123", 3)
+        hidden_product(0, grouped, [a0[:, 0, :], a123[:, 0, :], a123[:, 1, :], a123[:, 2, :]], (1, 2, 3, 0))
+
+        least23 = keep.tile([P, 2, HALF], F32, name="least23", tag="xc0_codes", align_bytes=64)
+        a123_sb = keep.tile([P, 3, HALF], F32, name="a123_sb")
+        code_and_upper(1, 1, buf_x[:, 0, :], buf_x[:, 1, :], least01[:, 1, slots(1)])
+        larger_pair(grouped, 0, least01[:, :, slots(1)], lower01[:, :, slots(1)])
+        code_and_upper(2, 1, buf_y[:, 0, :], buf_y[:, 1, :], least23[:, 0, :])
+        lower(2, 1, buf_z[:, 0, :])
+        nc.vector.tensor_copy(a123_sb[:], a123[:])
+        code_and_upper(3, 1, buf_x[:, 0, :], buf_x[:, 1, :], least23[:, 1, :])
+        lower(3, 1, buf_z[:, 1, :])
+        larger_pair(grouped, 1, least23[:], buf_z[:])
+        b01, b23 = bank("b01", 2), bank("b23", 2)
+        hidden_product(1, grouped, [b01[:, 0, :], b01[:, 1, :], b23[:, 0, :], b23[:, 1, :]], range(PACK))
+
+        nc.vector.tensor_copy(least23[:, 0, :], a0[:, 0, :])
+        for t in (1, 2, 3):
+            put_scalar(t, 0, a123_sb[:, t - 1, :])
+        put_vector(0, 0, least23[:, 0, :])
+
+        b01_sb = pair_tile("b01_sb")
+        b23_sb = keep.tile([P, 2, HALF], F32, name="b23_sb", align_bytes=64)
+        nc.vector.tensor_copy(b01_sb[:], b01[:])
+        nc.vector.tensor_copy(b23_sb[:], b23[:])
+        put_scalar(0, 1, b01_sb[:, 0, :])
+        put_vector(1, 1, b01_sb[:, 1, :])
+        put_vector(2, 1, b23_sb[:, 0, :])
+        put_vector(3, 1, b23_sb[:, 1, :])
+
+        hid_grouped = keep.tile([P, O, PACK], BF16, name="hid_grouped", tag="b23_sb", align_bytes=64)
+        for pair in range(2):
+            first = keep.tile([P, 2, O], F32, name="first" + str(pair))
+            second = keep.tile([P, 2, O], F32, name="second" + str(pair))
+            for t in (2 * pair, 2 * pair + 1):
+                fetch(first[:, t % 2, :], board[t], first_list[:], sa_sb[:, t : t + 1])
+                fetch(second[:, t % 2, :], board[t], second_list[:], sb_sb[:, t : t + 1])
+            larger_pair(hid_grouped, pair, first[:], second[:])
+        hid_codes, hid_scale = quantise("hid", hid_grouped)
+
+        for u in range(N // P):
+            acc = psum.tile([P, O], F32, name="result" + str(u))
+            nc.tensor.matmul_mx(
+                out=acc[:],
+                lhsT=wb_codes[:, P * u : P * (u + 1)].bitcast(FP8X4),
+                lhsT_scale=wb_scale[:, P * u : P * (u + 1)],
+                rhs=hid_codes[:].bitcast(FP8X4),
+                rhs_scale=hid_scale[:],
+                start=True,
+                stop=True,
+            )
+            result = keep.tile([P, O], F32, name="result_sb" + str(u))
+            if u == 0:
+                nc.vector.tensor_copy(result[:], acc[:])
+                nc.sync.dma_start(out[P * u : P * (u + 1), :], result[:])
+            else:
+                nc.scalar.copy(result[:], acc[:])
+                nc.scalar.dma_start(out[P * u : P * (u + 1), :], result[:])

@@ -83,6 +83,11 @@ def tile_picked_boundedcode_store_one_boardmixed_one_plain_kernel(
                 wb_scale[32 * q : 32 * q + 4, :].bitcast(I32), wb_scales[0, 4 * q : 4 * q + 4, :].bitcast(I32)
             )
 
+        warm_in = keep.tile([P, 1], F32, name="warm_in")
+        warm_out = keep.tile([P, 1], F32, name="warm_out")
+        nc.vector.memset(warm_in[:], 0.0)
+        nc.scalar.activation(out=warm_out[:], in_=warm_in[:], func=COPY)
+
         board = [keep.tile([P, C], F32, name="board" + str(t)) for t in range(PACK)]
         for t in range(PACK):
             nc.vector.memset(board[t][:], 0.0)

@@ -37,9 +37,9 @@ def tile_picked_boundedcode_store_one_boardmixed_one_plain_kernel(
             nc.sync.dma_start(tile[:], src)
             return tile
 
-        def load_factors(name, src, queue=nc.sync):
-            tile = keep.tile([P, PACK], F32, name=name)
-            queue.dma_start(tile[:], src.rearrange("(p t) o -> p (t o)", t=PACK))
+        def load_factors(name, src, tag=""):
+            tile = keep.tile([P, PACK], F32, name=name, tag=tag or name)
+            nc.sync.dma_start(tile[:], src.rearrange("(p t) o -> p (t o)", t=PACK))
             return tile
 
         def load_rows(name, src, t, queue=nc.sync):
@@ -47,41 +47,44 @@ def tile_picked_boundedcode_store_one_boardmixed_one_plain_kernel(
             queue.dma_start(tile[:], src.rearrange("(p t) c -> p t c", t=PACK)[:, t, :])
             return tile
 
-        wt_scale_window = keep.tile([P, F], U8, name="wt_scale_window")
-        wb_scale = keep.tile([P, N], U8, name="wb_scale", align_bytes=64)
-        nc.vector.memset(wt_scale_window[:].bitcast(I32), 0)
-        nc.vector.memset(wb_scale[:].bitcast(I32), 0)
+        wt_scale_window = keep.tile([P, F], U8, name="wt_scale_window", align_bytes=64)
+        nc.gpsimd.memset(wt_scale_window[:].bitcast(I32), 0)
+        nc.gpsimd.dma_start(wt_scale_window[0:16, :].bitcast(I32), wt_scales[0].bitcast(I32))
+        wt_scale = keep.tile([P, R], U8, name="wt_scale", align_bytes=64)
+        nc.vector.memset(wt_scale[:].bitcast(I32), 0)
 
         ta_rows, tb_rows = {}, {}
         code_list = load_list("code_list", offs)
         ga_sb = load_factors("ga_sb", ga)
         ta_rows[0] = load_rows("ta_rows", ta, 0, nc.scalar)
-        wt_scale_stage = keep.tile([4, 4, F // 4], I32, name="wt_scale_stage")
-        nc.gpsimd.dma_start(wt_scale_stage[:], wt_scales[0].bitcast(I32).rearrange("(q r) c -> r q c", r=4))
+        ta_rows[1] = load_rows("ta_rows", ta, 1)
         upper_list = load_list("upper_list", offs2)
         gb_sb = load_factors("gb_sb", gb)
         tb_rows[0] = load_rows("tb_rows", tb, 0)
         store_list = load_list("store_list", offs4)
         wt_word_window = keep.tile([P, F], U16, name="wt_word_window")
         nc.sync.dma_start(wt_word_window[:].bitcast(I32), wt_words[0].bitcast(I32))
-        ta_rows[1] = load_rows("ta_rows", ta, 1)
+        tb_rows[1] = load_rows("tb_rows", tb, 1)
         lower_list = load_list("lower_list", offs3)
         gd_sb = load_factors("gd_sb", gd)
-        tb_rows[1] = load_rows("tb_rows", tb, 1)
-        for t in (2, 3):
+        for t in range(2, PACK):
             ta_rows[t] = load_rows("ta_rows", ta, t)
             tb_rows[t] = load_rows("tb_rows", tb, t)
+
+        wt_picked = keep.tile([P, R], U16, name="wt_picked", align_bytes=64)
+        wt_scale_picked = keep.tile([P, R], U8, name="wt_scale_picked")
+        nc.vector.tensor_copy(
+            wt_scale_picked[:].rearrange("p (t m) -> p m t", t=PACK), wt_scale_window[:].indirect(store_list[:])
+        )
+        nc.vector.tensor_copy(wt_picked[:], wt_word_window[:].indirect(store_list[:]))
+        for q in range(4):
+            nc.sync.dma_start(
+                wt_scale[32 * q : 32 * q + 4, :].bitcast(I32), wt_scale_picked[4 * q : 4 * q + 4, :].bitcast(I32)
+            )
+
         board_list = load_list("board_list", offs5)
         first_list = load_list("first_list", offs6)
         second_list = load_list("second_list", offs7)
-        sa_sb = load_factors("sa_sb", sa)
-        sb_sb = load_factors("sb_sb", sb)
-        wb_codes = keep.tile([P, N], U32, name="wb_codes", align_bytes=64)
-        nc.sync.dma_start(wb_codes[:].bitcast(I32), wb_words[0].rearrange("p n r -> p (n r)").bitcast(I32))
-        for q in range(4):
-            nc.sync.dma_start(
-                wb_scale[32 * q : 32 * q + 4, :].bitcast(I32), wb_scales[0, 4 * q : 4 * q + 4, :].bitcast(I32)
-            )
 
         warm_in = keep.tile([P, 1], F32, name="warm_in")
         warm_out = keep.tile([P, 1], F32, name="warm_out")
@@ -90,7 +93,7 @@ def tile_picked_boundedcode_store_one_boardmixed_one_plain_kernel(
 
         board = [keep.tile([P, C], F32, name="board" + str(t)) for t in range(PACK)]
         for t in range(PACK):
-            nc.vector.memset(board[t][:], 0.0)
+            nc.gpsimd.memset(board[t][:], 0.0)
 
         def fetch(dst, window, offsets, factor):
             nc.scalar.activation(out=dst, in_=window[:].indirect(offsets), func=COPY, scale=factor)
@@ -121,12 +124,10 @@ def tile_picked_boundedcode_store_one_boardmixed_one_plain_kernel(
         def quantise(name, src):
             codes = keep.tile([P, HALF], U32, name=name + "_codes", align_bytes=64)
             scale = keep.tile([P, HALF], U8, name=name + "_scale", align_bytes=64)
-            nc.vector.quantize_mx(out=codes[:].bitcast(FP8X4), scales=scale[:], in_=src[:].rearrange("p j t -> p (j t)"))
+            nc.vector.quantize_mx(out=codes[:].bitcast(FP8X4), scales=scale[:], in_=src.rearrange("p j t -> p (j t)"))
             return codes, scale
 
-        wt_picked = keep.tile([P, R], U16, name="wt_picked")
         wt_codes = keep.tile([P, R], U16, name="wt_codes", align_bytes=64)
-        wt_scale = keep.tile([P, R], U8, name="wt_scale", align_bytes=64)
 
         def hidden_product(h, grouped, sums, order):
             codes, scale = quantise("xc" + str(h), grouped)
@@ -151,55 +152,60 @@ def tile_picked_boundedcode_store_one_boardmixed_one_plain_kernel(
             return psum.tile([P, planes, HALF], F32, name=name)
 
         least01 = keep.tile([P, 2, J], F32, name="least01")
-        grouped = keep.tile([P, HALF, PACK], BF16, name="grouped", align_bytes=64)
+        grouped = keep.tile([P, J, PACK], BF16, name="grouped", align_bytes=64)
 
-        for q in range(4):
-            nc.vector.tensor_copy(wt_scale_window[32 * q : 32 * q + 4, :].bitcast(I32), wt_scale_stage[:, q, :])
-        nc.vector.tensor_copy(
-            wt_scale[:].rearrange("p (t m) -> p m t", t=PACK), wt_scale_window[:].indirect(store_list[:])
-        )
-        nc.vector.tensor_copy(wt_picked[:], wt_word_window[:].indirect(store_list[:]))
-
-        code0 = keep.tile([P, J], F32, name="code0")
-        upper0 = keep.tile([P, J], F32, name="upper0")
         lower01 = keep.tile([P, 2, J], F32, name="lower01")
-        fetch(code0[:], ta_rows[0], code_list[:], ga_sb[:, 0:1])
-        fetch(upper0[:], tb_rows[0], upper_list[:], gb_sb[:, 0:1])
-        fetch(lower01[:, 0, :], tb_rows[0], lower_list[:], gd_sb[:, 0:1])
-        nc.vector.tensor_tensor(least01[:, 0, :], code0[:], upper0[:], MIN)
+        code01 = keep.tile([P, 2, J], F32, name="code01")
+        upper01 = keep.tile([P, 2, J], F32, name="upper01")
+        for t in (0, 1):
+            fetch(code01[:, t, :], ta_rows[t], code_list[:], ga_sb[:, t : t + 1])
+        for t in (0, 1):
+            fetch(upper01[:, t, :], tb_rows[t], upper_list[:], gb_sb[:, t : t + 1])
+        for t in (0, 1):
+            fetch(lower01[:, t, :], tb_rows[t], lower_list[:], gd_sb[:, t : t + 1])
+        nc.vector.tensor_tensor(least01[:], code01[:], upper01[:], MIN)
         nc.vector.tensor_copy(
             wt_codes[:].rearrange("p (t m) -> p t m", t=PACK), wt_picked[:].rearrange("p (m t) -> p t m", t=PACK)
         )
-        buf_x, buf_y, buf_z = pair_tile("buf_x"), pair_tile("buf_y"), pair_tile("buf_z")
-        both1, both2 = pair_tile("both1"), pair_tile("both2")
-        code_and_upper(1, 0, both1[:, 0, :], both1[:, 1, :], least01[:, 1, slots(0)])
-        fetch(lower01[:, 1, :], tb_rows[1], lower_list[:], gd_sb[:, 1:2])
-        larger_pair(grouped, 0, least01[:, :, slots(0)], lower01[:, :, slots(0)])
-        code_and_upper(2, 0, both2[:, 0, :], both2[:, 1, :], buf_z[:, 0, :])
+        larger_pair(grouped[:], 0, least01[:], lower01[:])
+
+        wb_scale = keep.tile([P, N], U8, name="wb_scale", tag="wt_scale_window", align_bytes=64)
+        nc.vector.memset(wb_scale[:].bitcast(I32), 0)
+        for q in range(4):
+            nc.sync.dma_start(
+                wb_scale[32 * q : 32 * q + 4, :].bitcast(I32), wb_scales[0, 4 * q : 4 * q + 4, :].bitcast(I32)
+            )
+        wb_codes = keep.tile([P, N], U32, name="wb_codes", tag="wt_picked", align_bytes=64)
+        nc.sync.dma_start(wb_codes[:].bitcast(I32), wb_words[0].rearrange("p n r -> p (n r)").bitcast(I32))
+
+        buf_w, buf_x, buf_y, buf_z = pair_tile("buf_w"), pair_tile("buf_x"), pair_tile("buf_y"), pair_tile("buf_z")
+        code_and_upper(2, 0, buf_w[:, 0, :], buf_w[:, 1, :], buf_z[:, 0, :])
         lower(2, 0, buf_y[:, 0, :])
         code_and_upper(3, 0, buf_x[:, 0, :], buf_x[:, 1, :], buf_z[:, 1, :])
         lower(3, 0, buf_y[:, 1, :])
-        larger_pair(grouped, 1, buf_z[:], buf_y[:])
-        a0, a123 = bank("a0", 1), bank("a123", 3)
-        hidden_product(0, grouped, [a0[:, 0, :], a123[:, 0, :], a123[:, 1, :], a123[:, 2, :]], (1, 2, 3, 0))
+        larger_pair(grouped[:, slots(0), :], 1, buf_z[:], buf_y[:])
+        a1, a023 = bank("a1", 1), bank("a023", 3)
+        hidden_product(0, grouped[:, slots(0), :], [a023[:, 0, :], a1[:, 0, :], a023[:, 1, :], a023[:, 2, :]], (1, 2, 3, 0))
 
-        least23 = keep.tile([P, 2, HALF], F32, name="least23", tag="xc0_codes", align_bytes=64)
-        a123_sb = keep.tile([P, 3, HALF], F32, name="a123_sb")
-        code_and_upper(1, 1, buf_x[:, 0, :], buf_x[:, 1, :], least01[:, 1, slots(1)])
-        larger_pair(grouped, 0, least01[:, :, slots(1)], lower01[:, :, slots(1)])
-        code_and_upper(2, 1, buf_y[:, 0, :], buf_y[:, 1, :], least23[:, 0, :])
-        lower(2, 1, buf_z[:, 0, :])
-        nc.vector.tensor_copy(a123_sb[:], a123[:])
-        code_and_upper(3, 1, buf_x[:, 0, :], buf_x[:, 1, :], least23[:, 1, :])
-        lower(3, 1, buf_z[:, 1, :])
-        larger_pair(grouped, 1, least23[:], buf_z[:])
+        least23 = pair_tile("least23")
+        code_and_upper(2, 1, buf_x[:, 0, :], buf_x[:, 1, :], least23[:, 0, :])
+        lower(2, 1, buf_y[:, 0, :])
+        code_and_upper(3, 1, buf_z[:, 0, :], buf_z[:, 1, :], least23[:, 1, :])
+        lower(3, 1, buf_y[:, 1, :])
+        larger_pair(grouped[:, slots(1), :], 1, least23[:], buf_y[:])
+        sa_sb = load_factors("sa_sb", sa, tag="ga_sb")
+        sb_sb = load_factors("sb_sb", sb, tag="gb_sb")
+        a1_sb = keep.tile([P, HALF], F32, name="a1_sb")
+        a023_sb = keep.tile([P, 3, HALF], F32, name="a023_sb")
+        nc.scalar.copy(a1_sb[:], a1[:, 0, :])
+        nc.vector.tensor_copy(a023_sb[:], a023[:])
         b01, b23 = bank("b01", 2), bank("b23", 2)
-        hidden_product(1, grouped, [b01[:, 0, :], b01[:, 1, :], b23[:, 0, :], b23[:, 1, :]], range(PACK))
+        hidden_product(1, grouped[:, slots(1), :], [b01[:, 0, :], b01[:, 1, :], b23[:, 0, :], b23[:, 1, :]], range(PACK))
 
-        nc.vector.tensor_copy(least23[:, 0, :], a0[:, 0, :])
-        for t in (1, 2, 3):
-            put_scalar(t, 0, a123_sb[:, t - 1, :])
-        put_vector(0, 0, least23[:, 0, :])
+        put_scalar(1, 0, a1_sb[:])
+        put_scalar(2, 0, a023_sb[:, 1, :])
+        put_scalar(3, 0, a023_sb[:, 2, :])
+        put_vector(0, 0, a023_sb[:, 0, :])
 
         b01_sb = pair_tile("b01_sb")
         b23_sb = keep.tile([P, 2, HALF], F32, name="b23_sb", align_bytes=64)
@@ -217,8 +223,8 @@ def tile_picked_boundedcode_store_one_boardmixed_one_plain_kernel(
             for t in (2 * pair, 2 * pair + 1):
                 fetch(first[:, t % 2, :], board[t], first_list[:], sa_sb[:, t : t + 1])
                 fetch(second[:, t % 2, :], board[t], second_list[:], sb_sb[:, t : t + 1])
-            larger_pair(hid_grouped, pair, first[:], second[:])
-        hid_codes, hid_scale = quantise("hid", hid_grouped)
+            larger_pair(hid_grouped[:], pair, first[:], second[:])
+        hid_codes, hid_scale = quantise("hid", hid_grouped[:])
 
         for u in range(N // P):
             acc = psum.tile([P, O], F32, name="result" + str(u))

@@ -62,9 +62,9 @@ def tile_picked_boundedcode_store_one_boardmixed_one_plain_kernel(
         gb_sb = load_factors("gb_sb", gb)
         tb_rows[0] = load_rows("tb_rows", tb, 0)
         store_list = load_list("store_list", offs4)
+        tb_rows[1] = load_rows("tb_rows", tb, 1)
         wt_word_window = keep.tile([P, F], U16, name="wt_word_window")
         nc.sync.dma_start(wt_word_window[:].bitcast(I32), wt_words[0].bitcast(I32))
-        tb_rows[1] = load_rows("tb_rows", tb, 1)
         lower_list = load_list("lower_list", offs3)
         gd_sb = load_factors("gd_sb", gd)
         for t in range(2, PACK):
@@ -152,7 +152,7 @@ def tile_picked_boundedcode_store_one_boardmixed_one_plain_kernel(
             return psum.tile([P, planes, HALF], F32, name=name)
 
         least01 = keep.tile([P, 2, J], F32, name="least01")
-        grouped = keep.tile([P, J, PACK], BF16, name="grouped", align_bytes=64)
+        grouped = keep.tile([P, HALF, PACK], BF16, name="grouped", align_bytes=64)
 
         lower01 = keep.tile([P, 2, J], F32, name="lower01")
         code01 = keep.tile([P, 2, J], F32, name="code01")
@@ -167,7 +167,7 @@ def tile_picked_boundedcode_store_one_boardmixed_one_plain_kernel(
         nc.vector.tensor_copy(
             wt_codes[:].rearrange("p (t m) -> p t m", t=PACK), wt_picked[:].rearrange("p (m t) -> p t m", t=PACK)
         )
-        larger_pair(grouped[:], 0, least01[:], lower01[:])
+        larger_pair(grouped[:], 0, least01[:, :, slots(0)], lower01[:, :, slots(0)])
 
         wb_scale = keep.tile([P, N], U8, name="wb_scale", tag="wt_scale_window", align_bytes=64)
         nc.vector.memset(wb_scale[:].bitcast(I32), 0)
@@ -183,16 +183,17 @@ def tile_picked_boundedcode_store_one_boardmixed_one_plain_kernel(
         lower(2, 0, buf_y[:, 0, :])
         code_and_upper(3, 0, buf_x[:, 0, :], buf_x[:, 1, :], buf_z[:, 1, :])
         lower(3, 0, buf_y[:, 1, :])
-        larger_pair(grouped[:, slots(0), :], 1, buf_z[:], buf_y[:])
+        larger_pair(grouped[:], 1, buf_z[:], buf_y[:])
         a1, a023 = bank("a1", 1), bank("a023", 3)
-        hidden_product(0, grouped[:, slots(0), :], [a023[:, 0, :], a1[:, 0, :], a023[:, 1, :], a023[:, 2, :]], (1, 2, 3, 0))
+        hidden_product(0, grouped[:], [a023[:, 0, :], a1[:, 0, :], a023[:, 1, :], a023[:, 2, :]], (1, 2, 3, 0))
 
+        larger_pair(grouped[:], 0, least01[:, :, slots(1)], lower01[:, :, slots(1)])
         least23 = pair_tile("least23")
         code_and_upper(2, 1, buf_x[:, 0, :], buf_x[:, 1, :], least23[:, 0, :])
         lower(2, 1, buf_y[:, 0, :])
         code_and_upper(3, 1, buf_z[:, 0, :], buf_z[:, 1, :], least23[:, 1, :])
         lower(3, 1, buf_y[:, 1, :])
-        larger_pair(grouped[:, slots(1), :], 1, least23[:], buf_y[:])
+        larger_pair(grouped[:], 1, least23[:], buf_y[:])
         sa_sb = load_factors("sa_sb", sa, tag="ga_sb")
         sb_sb = load_factors("sb_sb", sb, tag="gb_sb")
         a1_sb = keep.tile([P, HALF], F32, name="a1_sb")
@@ -200,7 +201,7 @@ def tile_picked_boundedcode_store_one_boardmixed_one_plain_kernel(
         nc.scalar.copy(a1_sb[:], a1[:, 0, :])
         nc.vector.tensor_copy(a023_sb[:], a023[:])
         b01, b23 = bank("b01", 2), bank("b23", 2)
-        hidden_product(1, grouped[:, slots(1), :], [b01[:, 0, :], b01[:, 1, :], b23[:, 0, :], b23[:, 1, :]], range(PACK))
+        hidden_product(1, grouped[:], [b01[:, 0, :], b01[:, 1, :], b23[:, 0, :], b23[:, 1, :]], range(PACK))
 
         put_scalar(1, 0, a1_sb[:])
         put_scalar(2, 0, a023_sb[:, 1, :])

from contextlib import ExitStack

import concourse.mybir as mybir

K, J, R, T, F, C, O, N = 512, 256, 512, 512, 1024, 512, 128, 256
FLOPS = 2 * K * R * J + 2 * R * N * O

F32 = mybir.dt.float32
BF16 = mybir.dt.bfloat16
I32 = mybir.dt.int32
U32 = mybir.dt.uint32
U16 = mybir.dt.uint16
U8 = mybir.dt.uint8
FP8X4 = mybir.dt.float8_e4m3fn_x4
FP4X4 = mybir.dt.float4_e2m1fn_x4
COPY = mybir.ActivationFunctionType.Copy
MIN = mybir.AluOpType.min
MAX = mybir.AluOpType.max

P = 128
PACK = 4
HALF = J // 2
LIST_ROWS = 16


def tile_picked_boundedcode_store_one_boardmixed_one_plain_kernel(
    tc, ta, tb, ga, gb, gd, wt_words, wt_scales, sa, sb, wb_words, wb_scales,
    offs, offs2, offs3, offs4, offs5, offs6, offs7, out,
):
    nc = tc.nc
    with ExitStack() as ctx:
        keep = ctx.enter_context(tc.tile_pool(name="keep", bufs=1))
        psum = ctx.enter_context(tc.psum_pool(name="psum", bufs=1))

        def load_list(name, src):
            tile = keep.tile(list(src.shape), U16, name=name)
            nc.sync.dma_start(tile[:], src)
            return tile

        def load_factors(name, src, tag=""):
            tile = keep.tile([P, PACK], F32, name=name, tag=tag or name)
            nc.sync.dma_start(tile[:], src.rearrange("(p t) o -> p (t o)", t=PACK))
            return tile

        def load_rows(name, src, t, queue=nc.sync):
            tile = keep.tile([P, T], F32, name=name + str(t))
            queue.dma_start(tile[:], src.rearrange("(p t) c -> p t c", t=PACK)[:, t, :])
            return tile

        wt_scale_window = keep.tile([P, F], U8, name="wt_scale_window", align_bytes=64)
        nc.gpsimd.memset(wt_scale_window[:].bitcast(I32), 0)
        nc.gpsimd.dma_start(wt_scale_window[0:16, :].bitcast(I32), wt_scales[0].bitcast(I32))
        wt_scale = keep.tile([P, R], U8, name="wt_scale", align_bytes=64)
        nc.vector.memset(wt_scale[:].bitcast(I32), 0)

        ta_rows, tb_rows = {}, {}
        code_list = load_list("code_list", offs)
        ga_sb = load_factors("ga_sb", ga)
        ta_rows[0] = load_rows("ta_rows", ta, 0, nc.scalar)
        ta_rows[1] = load_rows("ta_rows", ta, 1)
        upper_list = load_list("upper_list", offs2)
        gb_sb = load_factors("gb_sb", gb)
        tb_rows[0] = load_rows("tb_rows", tb, 0)
        store_list = load_list("store_list", offs4)
        tb_rows[1] = load_rows("tb_rows", tb, 1)
        wt_word_window = keep.tile([P, F], U16, name="wt_word_window")
        nc.sync.dma_start(wt_word_window[:].bitcast(I32), wt_words[0].bitcast(I32))
        lower_list = load_list("lower_list", offs3)
        gd_sb = load_factors("gd_sb", gd)
        for t in range(2, PACK):
            ta_rows[t] = load_rows("ta_rows", ta, t)
            tb_rows[t] = load_rows("tb_rows", tb, t)

        wt_picked = keep.tile([P, R], U16, name="wt_picked", align_bytes=64)
        wt_scale_picked = keep.tile([P, R], U8, name="wt_scale_picked")
        nc.vector.tensor_copy(
            wt_scale_picked[:].rearrange("p (t m) -> p m t", t=PACK), wt_scale_window[:].indirect(store_list[:])
        )
        nc.vector.tensor_copy(wt_picked[:], wt_word_window[:].indirect(store_list[:]))
        for q in range(4):
            nc.sync.dma_start(
                wt_scale[32 * q : 32 * q + 4, :].bitcast(I32), wt_scale_picked[4 * q : 4 * q + 4, :].bitcast(I32)
            )

        board_list = load_list("board_list", offs5)
        first_list = load_list("first_list", offs6)
        second_list = load_list("second_list", offs7)

        warm_in = keep.tile([P, 1], F32, name="warm_in")
        warm_out = keep.tile([P, 1], F32, name="warm_out")
        nc.vector.memset(warm_in[:], 0.0)
        nc.scalar.activation(out=warm_out[:], in_=warm_in[:], func=COPY)

        board = [keep.tile([P, C], F32, name="board" + str(t)) for t in range(PACK)]
        for t in range(PACK):
            nc.gpsimd.memset(board[t][:], 0.0)

        def fetch(dst, window, offsets, factor):
            nc.scalar.activation(out=dst, in_=window[:].indirect(offsets), func=COPY, scale=factor)

        def half_of(lst, h):
            cols = HALF // LIST_ROWS
            return lst[:, h * cols : (h + 1) * cols]

        def slots(h):
            return slice(h * HALF, (h + 1) * HALF)

        def pair_tile(name):
            return keep.tile([P, 2, HALF], F32, name=name)

        def code_and_upper(t, h, code, upper, least):
            fetch(code, ta_rows[t], half_of(code_list, h), ga_sb[:, t : t + 1])
            fetch(upper, tb_rows[t], half_of(upper_list, h), gb_sb[:, t : t + 1])
            nc.vector.tensor_tensor(least, code, upper, MIN)

        def lower(t, h, dst):
            fetch(dst, tb_rows[t], half_of(lower_list, h), gd_sb[:, t : t + 1])

        def larger_pair(dst, pair, x, y):
            nc.vector.tensor_tensor(
                dst[:, :, 2 * pair : 2 * pair + 2], x.rearrange("p t j -> p j t"), y.rearrange("p t j -> p j t"), MAX
            )

        def quantise(name, src):
            codes = keep.tile([P, HALF], U32, name=name + "_codes", align_bytes=64)
            scale = keep.tile([P, HALF], U8, name=name + "_scale", align_bytes=64)
            nc.vector.quantize_mx(out=codes[:].bitcast(FP8X4), scales=scale[:], in_=src.rearrange("p j t -> p (j t)"))
            return codes, scale

        wt_codes = keep.tile([P, R], U16, name="wt_codes", align_bytes=64)

        def hidden_product(h, grouped, sums, order):
            codes, scale = quantise("xc" + str(h), grouped)
            for t in order:
                nc.tensor.matmul_mx(
                    out=sums[t],
                    lhsT=wt_codes[:, P * t : P * (t + 1)].bitcast(FP4X4),
                    lhsT_scale=wt_scale[:, P * t : P * (t + 1)],
                    rhs=codes[:].bitcast(FP8X4),
                    rhs_scale=scale[:],
                    start=True,
                    stop=True,
                )

        def put_vector(t, h, values):
            nc.vector.tensor_copy(board[t][:].indirect(half_of(board_list, h)), values)

        def put_scalar(t, h, values):
            nc.scalar.activation(out=board[t][:].indirect(half_of(board_list, h)), in_=values, func=COPY)

        def bank(name, planes):
            return psum.tile([P, planes, HALF], F32, name=name)

        least01 = keep.tile([P, 2, J], F32, name="least01")
        grouped = keep.tile([P, HALF, PACK], BF16, name="grouped", align_bytes=64)

        lower01 = keep.tile([P, 2, J], F32, name="lower01")
        code01 = keep.tile([P, 2, J], F32, name="code01")
        upper01 = keep.tile([P, 2, J], F32, name="upper01")
        for t in (0, 1):
            fetch(code01[:, t, :], ta_rows[t], code_list[:], ga_sb[:, t : t + 1])
        for t in (0, 1):
            fetch(upper01[:, t, :], tb_rows[t], upper_list[:], gb_sb[:, t : t + 1])
        for t in (0, 1):
            fetch(lower01[:, t, :], tb_rows[t], lower_list[:], gd_sb[:, t : t + 1])
        nc.vector.tensor_tensor(least01[:], code01[:], upper01[:], MIN)
        nc.vector.tensor_copy(
            wt_codes[:].rearrange("p (t m) -> p t m", t=PACK), wt_picked[:].rearrange("p (m t) -> p t m", t=PACK)
        )
        larger_pair(grouped[:], 0, least01[:, :, slots(0)], lower01[:, :, slots(0)])

        wb_scale = keep.tile([P, N], U8, name="wb_scale", tag="wt_scale_window", align_bytes=64)
        nc.vector.memset(wb_scale[:].bitcast(I32), 0)
        for q in range(4):
            nc.sync.dma_start(
                wb_scale[32 * q : 32 * q + 4, :].bitcast(I32), wb_scales[0, 4 * q : 4 * q + 4, :].bitcast(I32)
            )
        wb_codes = keep.tile([P, N], U32, name="wb_codes", tag="wt_picked", align_bytes=64)
        nc.sync.dma_start(wb_codes[:].bitcast(I32), wb_words[0].rearrange("p n r -> p (n r)").bitcast(I32))

        buf_w, buf_x, buf_y, buf_z = pair_tile("buf_w"), pair_tile("buf_x"), pair_tile("buf_y"), pair_tile("buf_z")
        code_and_upper(2, 0, buf_w[:, 0, :], buf_w[:, 1, :], buf_z[:, 0, :])
        lower(2, 0, buf_y[:, 0, :])
        code_and_upper(3, 0, buf_x[:, 0, :], buf_x[:, 1, :], buf_z[:, 1, :])
        lower(3, 0, buf_y[:, 1, :])
        larger_pair(grouped[:], 1, buf_z[:], buf_y[:])
        a1, a023 = bank("a1", 1), bank("a023", 3)
        hidden_product(0, grouped[:], [a023[:, 0, :], a1[:, 0, :], a023[:, 1, :], a023[:, 2, :]], (1, 2, 3, 0))

        larger_pair(grouped[:], 0, least01[:, :, slots(1)], lower01[:, :, slots(1)])
        least23 = pair_tile("least23")
        code_and_upper(2, 1, buf_x[:, 0, :], buf_x[:, 1, :], least23[:, 0, :])
        lower(2, 1, buf_y[:, 0, :])
        code_and_upper(3, 1, buf_z[:, 0, :], buf_z[:, 1, :], least23[:, 1, :])
        lower(3, 1, buf_y[:, 1, :])
        larger_pair(grouped[:], 1, least23[:], buf_y[:])
        sa_sb = load_factors("sa_sb", sa, tag="ga_sb")
        sb_sb = load_factors("sb_sb", sb, tag="gb_sb")
        a1_sb = keep.tile([P, HALF], F32, name="a1_sb")
        a023_sb = keep.tile([P, 3, HALF], F32, name="a023_sb")
        nc.scalar.copy(a1_sb[:], a1[:, 0, :])
        nc.vector.tensor_copy(a023_sb[:], a023[:])
        b01, b23 = bank("b01", 2), bank("b23", 2)
        hidden_product(1, grouped[:], [b01[:, 0, :], b01[:, 1, :], b23[:, 0, :], b23[:, 1, :]], range(PACK))

        put_scalar(1, 0, a1_sb[:])
        put_scalar(2, 0, a023_sb[:, 1, :])
        put_scalar(3, 0, a023_sb[:, 2, :])
        put_vector(0, 0, a023_sb[:, 0, :])

        b01_sb = pair_tile("b01_sb")
        b23_sb = keep.tile([P, 2, HALF], F32, name="b23_sb", align_bytes=64)
        nc.vector.tensor_copy(b01_sb[:], b01[:])
        nc.vector.tensor_copy(b23_sb[:], b23[:])
        put_scalar(0, 1, b01_sb[:, 0, :])
        put_vector(1, 1, b01_sb[:, 1, :])
        put_vector(2, 1, b23_sb[:, 0, :])
        put_vector(3, 1, b23_sb[:, 1, :])

        hid_grouped = keep.tile([P, O, PACK], BF16, name="hid_grouped", tag="b23_sb", align_bytes=64)
        for pair in range(2):
            first = keep.tile([P, 2, O], F32, name="first" + str(pair))
            second = keep.tile([P, 2, O], F32, name="second" + str(pair))
            for t in (2 * pair, 2 * pair + 1):
                fetch(first[:, t % 2, :], board[t], first_list[:], sa_sb[:, t : t + 1])
                fetch(second[:, t % 2, :], board[t], second_list[:], sb_sb[:, t : t + 1])
            larger_pair(hid_grouped[:], pair, first[:], second[:])
        hid_codes, hid_scale = quantise("hid", hid_grouped[:])

        for u in range(N // P):
            acc = psum.tile([P, O], F32, name="result" + str(u))
            nc.tensor.matmul_mx(
                out=acc[:],
                lhsT=wb_codes[:, P * u : P * (u + 1)].bitcast(FP8X4),
                lhsT_scale=wb_scale[:, P * u : P * (u + 1)],
                rhs=hid_codes[:].bitcast(FP8X4),
                rhs_scale=hid_scale[:],
                start=True,
                stop=True,
            )
            result = keep.tile([P, O], F32, name="result_sb" + str(u))
            if u == 0:
                nc.vector.tensor_copy(result[:], acc[:])
                nc.sync.dma_start(out[P * u : P * (u + 1), :], result[:])
            else:
                nc.scalar.copy(result[:], acc[:])
                nc.scalar.dma_start(out[P * u : P * (u + 1), :], result[:])
